import numpy as np
import ml_dtypes


def mxq(x, axis, fmt="e4m3"):
    dtype, down = {"e4m3": (ml_dtypes.float8_e4m3fn, 7), "e5m2": (ml_dtypes.float8_e5m2, 14)}[fmt]
    v = np.moveaxis(np.asarray(x, np.float32).astype(ml_dtypes.bfloat16).astype(np.float64), axis, -1)
    blocks = v.reshape(v.shape[:-1] + (-1, 32))
    amax = np.abs(blocks).max(-1, keepdims=True)
    byte = np.maximum(np.where(amax > 0, np.frexp(amax)[1] - 1 + 127, 0) - down, 1)
    scale = np.exp2(byte - 127.0)
    codes = (blocks / scale).astype(np.float32).astype(dtype).astype(np.float64)
    return np.moveaxis((codes * scale).reshape(v.shape), -1, axis)


WIDE = False


def mx_kscale(k):
    if not WIDE:
        return np.ones(k)
    levels = np.array([10, -10, 5, -5, 0])
    if k % 512:
        return np.exp2(np.random.permutation(np.resize(levels, k // 32))).repeat(32)
    a = np.empty((k // 512, 16))
    for p in range(k // 512):
        a[p, :8] = np.random.permutation(np.resize(levels, 8))
        for g in range(8):
            far = levels[np.abs(levels - a[p, g]) >= 10]
            a[p, g + 8] = far[np.random.randint(len(far))]
    return np.exp2(a.ravel()).repeat(32)


def f64(x):
    return np.asarray(x).astype(np.float64)


def striped(idx):
    return np.tile(np.asarray(idx).reshape(-1, 16).T, (8, 1)).astype(np.uint16)


def unstriped(offs):
    return offs[:16].T.reshape(-1).astype(np.int64)


def striped8(idx):
    return np.asarray(idx).reshape(8, -1, 16).transpose(0, 2, 1).reshape(128, -1).astype(np.uint16)


def unstriped8(offs):
    return offs.reshape(8, 16, -1).transpose(0, 2, 1).reshape(8, -1).astype(np.int64)


def pick8(x, idx, run):
    r = np.arange(len(x))
    return x[r[:, None], idx[r % (8 * run) // run]]


E2M1 = np.array([0.0, 0.5, 1.0, 1.5, 2.0, 3.0, 4.0, 6.0, -0.0, -0.5, -1.0, -1.5, -2.0, -3.0, -4.0, -6.0])


def pack_weight(w, fmt):
    k, n = w.shape
    w = f64(np.asarray(w, np.float32).astype(ml_dtypes.bfloat16)).reshape(k // 32, 32, n)
    amax = np.abs(w).max(1)
    if fmt == "e4m3":
        byte = np.frexp(amax)[1] - 1 + 127 - 7
    else:
        mant, ex = np.frexp(amax / 6.0)
        byte = np.where(mant > 0.5, ex, ex - 1) + 127
    byte = np.clip(np.where(amax > 0, byte, 1), 1, 254)
    scaled = (w * np.exp2(127.0 - byte)[:, None, :]).reshape(k, n).astype(np.float32)
    by_word = np.ascontiguousarray(scaled.reshape(k // 512, 128, 4, n).transpose(0, 1, 3, 2))
    if fmt == "e4m3":
        words = by_word.astype(ml_dtypes.float8_e4m3fn).view(np.uint8)
    else:
        c = by_word.astype(ml_dtypes.float4_e2m1fn).view(np.uint8) & 0xF
        words = (c[..., 0::2] | (c[..., 1::2] << 4)).reshape(k // 512, 128, 2 * n)
    return np.ascontiguousarray(words), np.ascontiguousarray(byte.astype(np.uint8).reshape(k // 512, 16, n))


def unpack_weight(words, scales, fmt):
    g, _, n = scales.shape
    words = np.ascontiguousarray(words).reshape(g, 128, n, -1)
    if fmt == "e4m3":
        vals = words.view(ml_dtypes.float8_e4m3fn).astype(np.float64)
    else:
        nib = np.empty((g, 128, n, 4), np.uint8)
        nib[..., 0::2] = words & 0xF
        nib[..., 1::2] = words >> 4
        vals = E2M1[nib]
    vals = vals * np.repeat(np.exp2(scales.astype(np.float64) - 127.0), 8, axis=1)[..., None]
    return vals.transpose(0, 1, 3, 2).reshape(g * 512, n)


K, J, R, T, U, F, C, O, S, N = 512, 256, 512, 1024, 512, 1024, 512, 128, 256, 256


def setup_inputs():
    n = np.random.standard_normal
    idx = np.stack([np.random.permutation(T)[:U] for _ in range(8)])
    idx2 = np.random.permutation(U)[:J]
    idx3 = np.random.permutation(F)[:R]
    idx4 = np.stack([np.random.permutation(C)[:J] for _ in range(8)])
    idx5 = np.stack([np.random.permutation(C)[:S] for _ in range(8)])
    idx6 = np.random.permutation(C)[:S]
    idx7 = np.stack([np.random.permutation(S)[:O] for _ in range(8)])
    fk = mx_kscale(K)
    fr = mx_kscale(R)
    tr = np.ones(F)
    tr[idx3] = fr
    wtp = pack_weight(n((K, F)) * 1 / np.sqrt(K) / fk[:, None] * tr, "e2m1")
    wbp = pack_weight(n((R, N)) * 1 / np.sqrt(R) / fr[:, None], "e4m3")
    return {
        "ta": (np.random.randint(-7, 8, (K, T)).astype(np.float64)).astype(np.float32),
        "ga": ((np.random.randint(8, 25, (K, 1)) / 64.0) * fk[:, None]).astype(np.float32),
        "gb": (np.random.uniform(0.5, 1.6, (K, 1))).astype(np.float32),
        "wt_words": wtp[0],
        "wt_scales": wtp[1],
        "sa": (np.random.uniform(0.5, 1.6, (R, 1))).astype(np.float32),
        "sb": (np.random.uniform(0.5, 1.6, (R, 1))).astype(np.float32),
        "sd": (np.random.uniform(0.5, 1.6, (R, 1))).astype(np.float32),
        "wb_words": wbp[0],
        "wb_scales": wbp[1],
        "offs": striped8(idx),
        "offs2": striped(idx2),
        "offs3": striped(idx3),
        "offs4": striped8(idx4),
        "offs5": striped8(idx5),
        "offs6": striped(idx6),
        "offs7": striped8(idx7),
    }


def reference(ta, ga, gb, wt_words, wt_scales, sa, sb, sd, wb_words, wb_scales, offs, offs2, offs3, offs4, offs5, offs6, offs7):
    idx = unstriped8(offs)
    idx2 = unstriped(offs2)
    idx3 = unstriped(offs3)
    idx4 = unstriped8(offs4)
    idx5 = unstriped8(offs5)
    idx6 = unstriped(offs6)
    idx7 = unstriped8(offs7)
    wtu = unpack_weight(wt_words, wt_scales, "e2m1")
    wbu = unpack_weight(wb_words, wb_scales, "e4m3")
    xcd = pick8(f64(ta), idx, 64) * f64(ga)
    xc = xcd[:, idx2] * f64(gb)
    wtidx3g = wtu[:, idx3]
    xcq = mxq(xc, 0, "e4m3")
    a = wtidx3g.T @ xcq
    pw = np.zeros((R, C))
    pw[np.arange(R)[:, None], idx4[np.arange(R) % 512 // 64]] = a
    pg = np.maximum(pick8(pw, idx5, 64) * f64(sa), pw[:, idx6] * f64(sb))
    hid = pick8(pg, idx7, 64) * f64(sd)
    hidq = mxq(hid, 0, "e4m3")
    y = wbu.T @ hidq
    return y

@@ -1,0 +1,183 @@
+from contextlib import ExitStack
+
+import concourse.mybir as mybir
+
+K, J, R, T, U, F, C, O, S, N = 512, 256, 512, 1024, 512, 1024, 512, 128, 256, 256
+FLOPS = 2 * K * R * J + 2 * R * N * O
+
+F32 = mybir.dt.float32
+BF16 = mybir.dt.bfloat16
+I32 = mybir.dt.int32
+U32 = mybir.dt.uint32
+U16 = mybir.dt.uint16
+U8 = mybir.dt.uint8
+FP8X4 = mybir.dt.float8_e4m3fn_x4
+FP4X4 = mybir.dt.float4_e2m1fn_x4
+COPY = mybir.ActivationFunctionType.Copy
+MAX = mybir.AluOpType.max
+
+P = 128
+PACK = 4
+QUADS = 4
+LANES = 16
+HALF = J // 2
+
+
+def tile_picked_respelled_store_one_ladder_one_plain_kernel(
+    tc, ta, ga, gb, wt_words, wt_scales, sa, sb, sd, wb_words, wb_scales,
+    offs, offs2, offs3, offs4, offs5, offs6, offs7, out,
+):
+    nc = tc.nc
+    with ExitStack() as ctx:
+        keep = ctx.enter_context(tc.tile_pool(name="keep", bufs=1))
+        psum = ctx.enter_context(tc.psum_pool(name="psum", bufs=1))
+
+        def load_list(name, source):
+            tile = keep.tile(list(source.shape), U16, name=name)
+            nc.sync.dma_start(tile[:], source)
+            return tile
+
+        def load_rowwise(name, source, queue):
+            tile = keep.tile([P, PACK], F32, name=name)
+            queue.dma_start(tile[:], source.rearrange("(p t) o -> p (t o)", t=PACK))
+            return tile
+
+        ta_rows = ta.rearrange("(p t) c -> p t c", t=PACK)
+
+        def load_ta(t):
+            tile = keep.tile([P, T], F32, name="ta%d" % t, tag="ta%d" % t, align_bytes=64)
+            nc.sync.dma_start(tile[:], ta_rows[:, t, :])
+            return tile
+
+        board = [keep.tile([P, C], F32, name="board%d" % t) for t in range(PACK)]
+        wt_scale_table = keep.tile([P, F], U8, name="wt_scale_table", align_bytes=64)
+        wb_scale = keep.tile([P, N], U8, name="wb_scale", align_bytes=64)
+        nc.vector.memset(wt_scale_table[:].bitcast(I32), 0)
+        nc.vector.memset(wb_scale[:].bitcast(I32), 0)
+        for t in range(PACK):
+            nc.vector.memset(board[t][:], 0.0)
+
+        list1 = load_list("list1", offs)
+        ga_t = load_rowwise("ga_t", ga, nc.scalar)
+        table = [load_ta(0), load_ta(1)]
+        list2 = load_list("list2", offs2)
+        gb_t = load_rowwise("gb_t", gb, nc.sync)
+        wt_scale_rows = keep.tile([4, QUADS, F // 4], I32, name="wt_scale_rows")
+        nc.sync.dma_start(wt_scale_rows[:], wt_scales[0].bitcast(I32).rearrange("(q i) c -> i q c", i=4))
+        list3 = load_list("list3", offs3)
+        wt_word_table = keep.tile([P, F], U16, name="wt_word_table", align_bytes=64)
+        nc.sync.dma_start(wt_word_table[:].bitcast(I32), wt_words[0].bitcast(I32))
+        table.extend([load_ta(2), load_ta(3)])
+        list4 = load_list("list4", offs4)
+        list5 = load_list("list5", offs5)
+        list6 = load_list("list6", offs6)
+        list7 = load_list("list7", offs7)
+        sa_t = load_rowwise("sa_t", sa, nc.sync)
+        sb_t = load_rowwise("sb_t", sb, nc.sync)
+        sd_t = load_rowwise("sd_t", sd, nc.sync)
+        wb_code = keep.tile([P, N], I32, name="wb_code", align_bytes=64)
+        nc.sync.dma_start(wb_code[:], wb_words[0].rearrange("p n t -> p (n t)").bitcast(I32))
+        for q in range(QUADS):
+            nc.sync.dma_start(
+                wb_scale[32 * q : 32 * q + 4, :].bitcast(I32), wb_scales[0, 4 * q : 4 * q + 4, :].bitcast(I32)
+            )
+
+        for q in range(QUADS):
+            nc.vector.tensor_copy(wt_scale_table[32 * q : 32 * q + 4, :].bitcast(I32), wt_scale_rows[:, q, :])
+        wt_scale = keep.tile([P, R], U8, name="wt_scale", align_bytes=64)
+        nc.vector.tensor_copy(
+            wt_scale[:].rearrange("p (t m) -> p m t", t=PACK), wt_scale_table[:].indirect(list3[:])
+        )
+        wt_picked = keep.tile([P, R], U16, name="wt_picked", align_bytes=64)
+        nc.vector.tensor_copy(wt_picked[:], wt_word_table[:].indirect(list3[:]))
+        wt_code = keep.tile([P, 2 * R], U8, name="wt_code", align_bytes=64)
+        nc.vector.tensor_copy(
+            wt_code[:].rearrange("p (t m b) -> p t m b", t=PACK, b=2),
+            wt_picked[:].bitcast(U8).rearrange("p (m t b) -> p t m b", t=PACK, b=2),
+        )
+
+        xcd = [keep.tile([P, U], F32, name="xcd%d" % t) for t in range(PACK)]
+
+        def fetch_xc(rows, t, h):
+            cols = slice(h * HALF // LANES, (h + 1) * HALF // LANES)
+            nc.scalar.activation(rows[:, t, :], xcd[t][:].indirect(list2[:, cols]), COPY, scale=gb_t[:, t : t + 1])
+
+        def quantize(name, rows, width):
+            grouped = keep.tile([P, width, PACK], BF16, name=name + "_grouped", align_bytes=64)
+            nc.vector.tensor_copy(
+                grouped[:].rearrange("p (c i) t -> p c t i", i=4), rows[:].rearrange("p t (c i) -> p c t i", i=4)
+            )
+            code = keep.tile([P, width], U32, name=name + "_code", align_bytes=64)
+            scale = keep.tile([P, width], U8, name=name + "_scale", align_bytes=64)
+            nc.vector.quantize_mx(code[:].bitcast(FP8X4), scale[:], grouped[:].rearrange("p c t -> p (c t)"))
+            return code, scale
+
+        hidden = keep.tile([P, PACK, J], F32, name="hidden")
+
+        def first_product(h, rows):
+            code, scale = quantize("xc%d" % h, rows, HALF)
+            first = psum.tile([P, HALF], F32, name="first%d" % h)
+            rest = psum.tile([P, PACK - 1, HALF], F32, name="rest%d" % h)
+            for t in range(PACK):
+                nc.tensor.matmul_mx(
+                    first[:] if t == 0 else rest[:, t - 1, :],
+                    lhsT=wt_code[:, 2 * P * t : 2 * P * (t + 1)].bitcast(FP4X4),
+                    lhsT_scale=wt_scale[:, P * t : P * (t + 1)],
+                    rhs=code[:].bitcast(FP8X4),
+                    rhs_scale=scale[:],
+                    start=True,
+                    stop=True,
+                )
+            cols = slice(h * HALF, (h + 1) * HALF)
+            nc.scalar.copy(hidden[:, 0, cols], first[:])
+            nc.scalar.copy(hidden[:, 1:, cols], rest[:])
+
+        xc_first = keep.tile([P, PACK, HALF], BF16, name="xc_first", align_bytes=64)
+        for t in range(PACK):
+            nc.scalar.activation(xcd[t][:], table[t][:].indirect(list1[:]), COPY, scale=ga_t[:, t : t + 1])
+            fetch_xc(xc_first, t, 0)
+        xc_second = keep.tile([P, PACK, HALF], BF16, name="xc_second", tag="ta3", align_bytes=64)
+        for t in range(PACK):
+            fetch_xc(xc_second, t, 1)
+        first_product(0, xc_first)
+        first_product(1, xc_second)
+
+        for h in range(2):
+            nc.vector.tensor_copy(
+                board[0][:].indirect(list4[:, h * HALF // LANES : (h + 1) * HALF // LANES]),
+                hidden[:, 0, h * HALF : (h + 1) * HALF],
+            )
+        for t in range(1, PACK):
+            nc.vector.tensor_copy(board[t][:].indirect(list4[:]), hidden[:, t, :])
+
+        own = keep.tile([P, PACK, S], F32, name="own")
+        shared = keep.tile([P, PACK, S], F32, name="shared")
+        for t in range(PACK):
+            nc.scalar.activation(own[:, t, :], board[t][:].indirect(list5[:]), COPY, scale=sa_t[:, t : t + 1])
+            nc.scalar.activation(shared[:, t, :], board[t][:].indirect(list6[:]), COPY, scale=sb_t[:, t : t + 1])
+        kept = [keep.tile([P, S], F32, name="kept%d" % t) for t in range(PACK)]
+        for t in range(PACK):
+            nc.vector.tensor_tensor(kept[t][:], own[:, t, :], shared[:, t, :], MAX)
+        hid = keep.tile([P, PACK, O], BF16, name="hid", align_bytes=64)
+        for t in range(PACK):
+            nc.scalar.activation(hid[:, t, :], kept[t][:].indirect(list7[:]), COPY, scale=sd_t[:, t : t + 1])
+
+        code, scale = quantize("hid", hid, O)
+        for b in range(N // P):
+            acc = psum.tile([P, O], F32, name="y%d" % b)
+            nc.tensor.matmul_mx(
+                acc[:],
+                lhsT=wb_code[:, P * b : P * (b + 1)].bitcast(FP8X4),
+                lhsT_scale=wb_scale[:, P * b : P * (b + 1)],
+                rhs=code[:].bitcast(FP8X4),
+                rhs_scale=scale[:],
+                start=True,
+                stop=True,
+            )
+            result = keep.tile([P, O], F32, name="result%d" % b)
+            if b == 0:
+                nc.vector.tensor_copy(result[:], acc[:])
+                nc.sync.dma_start(out[P * b : P * (b + 1), :], result[:])
+            else:
+                nc.scalar.copy(result[:], acc[:])
+                nc.scalar.dma_start(out[P * b : P * (b + 1), :], result[:])

@@ -57,6 +57,11 @@ def tile_picked_respelled_store_one_ladder_one_plain_kernel(
         for t in range(PACK):
             nc.vector.memset(board[t][:], 0.0)
 
+        warm_in = keep.tile([P, 1], F32, name="warm_in")
+        warm_out = keep.tile([P, 1], F32, name="warm_out")
+        nc.gpsimd.memset(warm_in[:], 0.0)
+        nc.scalar.activation(warm_out[:], warm_in[:], COPY)
+
         list1 = load_list("list1", offs)
         ga_t = load_rowwise("ga_t", ga, nc.scalar)
         table = [load_ta(0), load_ta(1)]

@@ -62,17 +62,18 @@ def tile_picked_respelled_store_one_ladder_one_plain_kernel(
         nc.gpsimd.memset(warm_in[:], 0.0)
         nc.scalar.activation(warm_out[:], warm_in[:], COPY)
 
+        table = [load_ta(0)]
         list1 = load_list("list1", offs)
         ga_t = load_rowwise("ga_t", ga, nc.scalar)
-        table = [load_ta(0), load_ta(1)]
-        list2 = load_list("list2", offs2)
-        gb_t = load_rowwise("gb_t", gb, nc.sync)
         wt_scale_rows = keep.tile([4, QUADS, F // 4], I32, name="wt_scale_rows")
         nc.sync.dma_start(wt_scale_rows[:], wt_scales[0].bitcast(I32).rearrange("(q i) c -> i q c", i=4))
         list3 = load_list("list3", offs3)
+        table.extend([load_ta(1), load_ta(2)])
         wt_word_table = keep.tile([P, F], U16, name="wt_word_table", align_bytes=64)
         nc.sync.dma_start(wt_word_table[:].bitcast(I32), wt_words[0].bitcast(I32))
-        table.extend([load_ta(2), load_ta(3)])
+        list2 = load_list("list2", offs2)
+        gb_t = load_rowwise("gb_t", gb, nc.sync)
+        table.append(load_ta(3))
         list4 = load_list("list4", offs4)
         list5 = load_list("list5", offs5)
         list6 = load_list("list6", offs6)
@@ -107,20 +108,17 @@ def tile_picked_respelled_store_one_ladder_one_plain_kernel(
             cols = slice(h * HALF // LANES, (h + 1) * HALF // LANES)
             nc.scalar.activation(rows[:, t, :], xcd[t][:].indirect(list2[:, cols]), COPY, scale=gb_t[:, t : t + 1])
 
-        def quantize(name, rows, width):
-            grouped = keep.tile([P, width, PACK], BF16, name=name + "_grouped", align_bytes=64)
-            nc.vector.tensor_copy(
-                grouped[:].rearrange("p (c i) t -> p c t i", i=4), rows[:].rearrange("p t (c i) -> p c t i", i=4)
-            )
-            code = keep.tile([P, width], U32, name=name + "_code", align_bytes=64)
+        def interleave(grouped, rows, pair, copy):
+            planes = slice(2 * pair, 2 * pair + 2)
+            copy(grouped[:, :, planes], rows[:, planes, :].rearrange("p t c -> p c t"))
+
+        def quantize(name, grouped, width, tag):
+            code = keep.tile([P, width], U32, name=name + "_code", tag=tag, align_bytes=64)
             scale = keep.tile([P, width], U8, name=name + "_scale", align_bytes=64)
             nc.vector.quantize_mx(code[:].bitcast(FP8X4), scale[:], grouped[:].rearrange("p c t -> p (c t)"))
             return code, scale
 
-        hidden = keep.tile([P, PACK, J], F32, name="hidden")
-
-        def first_product(h, rows):
-            code, scale = quantize("xc%d" % h, rows, HALF)
+        def first_product(h, code, scale):
             first = psum.tile([P, HALF], F32, name="first%d" % h)
             rest = psum.tile([P, PACK - 1, HALF], F32, name="rest%d" % h)
             for t in range(PACK):
@@ -133,26 +131,46 @@ def tile_picked_respelled_store_one_ladder_one_plain_kernel(
                     start=True,
                     stop=True,
                 )
-            cols = slice(h * HALF, (h + 1) * HALF)
-            nc.scalar.copy(hidden[:, 0, cols], first[:])
-            nc.scalar.copy(hidden[:, 1:, cols], rest[:])
+            return first, rest
 
-        xc_first = keep.tile([P, PACK, HALF], BF16, name="xc_first", align_bytes=64)
-        for t in range(PACK):
+        def scatter_half(t, h, values):
+            nc.vector.tensor_copy(board[t][:].indirect(list4[:, h * HALF // LANES : (h + 1) * HALF // LANES]), values)
+
+        hidden = keep.tile([P, PACK, J], F32, name="hidden")
+        early, late = slice(0, HALF), slice(HALF, J)
+
+        def spell(t):
             nc.scalar.activation(xcd[t][:], table[t][:].indirect(list1[:]), COPY, scale=ga_t[:, t : t + 1])
+
+        for t in range(PACK - 1):
+            spell(t)
+        xc_first = keep.tile([P, PACK, HALF], BF16, name="xc_first", tag="ta2", align_bytes=64)
+        for t in range(PACK - 1):
             fetch_xc(xc_first, t, 0)
+        spell(PACK - 1)
+        fetch_xc(xc_first, PACK - 1, 0)
         xc_second = keep.tile([P, PACK, HALF], BF16, name="xc_second", tag="ta3", align_bytes=64)
         for t in range(PACK):
             fetch_xc(xc_second, t, 1)
-        first_product(0, xc_first)
-        first_product(1, xc_second)
 
-        for h in range(2):
-            nc.vector.tensor_copy(
-                board[0][:].indirect(list4[:, h * HALF // LANES : (h + 1) * HALF // LANES]),
-                hidden[:, 0, h * HALF : (h + 1) * HALF],
-            )
-        for t in range(1, PACK):
+        grouped = keep.tile([P, HALF, PACK], BF16, name="xc0_grouped", tag="xc_grouped", align_bytes=64)
+        interleave(grouped, xc_first, 0, nc.vector.tensor_copy)
+        interleave(grouped, xc_first, 1, nc.vector.tensor_copy)
+        first, rest = first_product(0, *quantize("xc0", grouped, HALF, "xc0_code"))
+        grouped = keep.tile([P, HALF, PACK], BF16, name="xc1_grouped", tag="xc_grouped", align_bytes=64)
+        interleave(grouped, xc_second, 0, nc.vector.tensor_copy)
+        interleave(grouped, xc_second, 1, nc.scalar.copy)
+        opener = keep.tile([P, HALF], F32, name="opener", tag="opener", align_bytes=64)
+        nc.vector.tensor_copy(opener[:], first[:])
+        scatter_half(0, 0, opener[:])
+        nc.scalar.copy(hidden[:, 1:, early], rest[:])
+        first, rest = first_product(1, *quantize("xc1", grouped, HALF, "opener"))
+        nc.scalar.copy(hidden[:, 0, late], first[:])
+        nc.scalar.copy(hidden[:, 1:, late], rest[:])
+        scatter_half(1, 0, hidden[:, 1, early])
+        scatter_half(0, 1, hidden[:, 0, late])
+        scatter_half(1, 1, hidden[:, 1, late])
+        for t in range(2, PACK):
             nc.vector.tensor_copy(board[t][:].indirect(list4[:]), hidden[:, t, :])
 
         own = keep.tile([P, PACK, S], F32, name="own")
@@ -167,7 +185,10 @@ def tile_picked_respelled_store_one_ladder_one_plain_kernel(
         for t in range(PACK):
             nc.scalar.activation(hid[:, t, :], kept[t][:].indirect(list7[:]), COPY, scale=sd_t[:, t : t + 1])
 
-        code, scale = quantize("hid", hid, O)
+        grouped = keep.tile([P, O, PACK], BF16, name="hid_grouped", align_bytes=64)
+        interleave(grouped, hid, 0, nc.vector.tensor_copy)
+        interleave(grouped, hid, 1, nc.vector.tensor_copy)
+        code, scale = quantize("hid", grouped, O, "hid_code")
         for b in range(N // P):
             acc = psum.tile([P, O], F32, name="y%d" % b)
             nc.tensor.matmul_mx(

@@ -72,8 +72,11 @@ def tile_picked_respelled_store_one_ladder_one_plain_kernel(
         wt_word_table = keep.tile([P, F], U16, name="wt_word_table", align_bytes=64)
         nc.sync.dma_start(wt_word_table[:].bitcast(I32), wt_words[0].bitcast(I32))
         list2 = load_list("list2", offs2)
-        gb_t = load_rowwise("gb_t", gb, nc.sync)
+        gb_rows = gb.rearrange("(p t) o -> p (t o)", t=PACK)
+        gb_pair = [keep.tile([P, 2], F32, name="gb_pair%d" % u) for u in range(2)]
+        nc.sync.dma_start(gb_pair[0][:], gb_rows[:, 0:2])
         table.append(load_ta(3))
+        nc.sync.dma_start(gb_pair[1][:], gb_rows[:, 2:4])
         list4 = load_list("list4", offs4)
         list5 = load_list("list5", offs5)
         list6 = load_list("list6", offs6)
@@ -88,12 +91,6 @@ def tile_picked_respelled_store_one_ladder_one_plain_kernel(
                 wb_scale[32 * q : 32 * q + 4, :].bitcast(I32), wb_scales[0, 4 * q : 4 * q + 4, :].bitcast(I32)
             )
 
-        for q in range(QUADS):
-            nc.vector.tensor_copy(wt_scale_table[32 * q : 32 * q + 4, :].bitcast(I32), wt_scale_rows[:, q, :])
-        wt_scale = keep.tile([P, R], U8, name="wt_scale", align_bytes=64)
-        nc.vector.tensor_copy(
-            wt_scale[:].rearrange("p (t m) -> p m t", t=PACK), wt_scale_table[:].indirect(list3[:])
-        )
         wt_picked = keep.tile([P, R], U16, name="wt_picked", align_bytes=64)
         nc.vector.tensor_copy(wt_picked[:], wt_word_table[:].indirect(list3[:]))
         wt_code = keep.tile([P, 2 * R], U8, name="wt_code", align_bytes=64)
@@ -101,12 +98,18 @@ def tile_picked_respelled_store_one_ladder_one_plain_kernel(
             wt_code[:].rearrange("p (t m b) -> p t m b", t=PACK, b=2),
             wt_picked[:].bitcast(U8).rearrange("p (m t b) -> p t m b", t=PACK, b=2),
         )
+        for q in range(QUADS):
+            nc.vector.tensor_copy(wt_scale_table[32 * q : 32 * q + 4, :].bitcast(I32), wt_scale_rows[:, q, :])
+        wt_scale = keep.tile([P, R], U8, name="wt_scale", align_bytes=64)
+        nc.vector.tensor_copy(
+            wt_scale[:].rearrange("p (t m) -> p m t", t=PACK), wt_scale_table[:].indirect(list3[:])
+        )
 
         xcd = [keep.tile([P, U], F32, name="xcd%d" % t) for t in range(PACK)]
 
         def fetch_xc(rows, t, h):
             cols = slice(h * HALF // LANES, (h + 1) * HALF // LANES)
-            nc.scalar.activation(rows[:, t, :], xcd[t][:].indirect(list2[:, cols]), COPY, scale=gb_t[:, t : t + 1])
+            nc.scalar.activation(rows[:, t, :], xcd[t][:].indirect(list2[:, cols]), COPY, scale=gb_pair[t // 2][:, t % 2 : t % 2 + 1])
 
         def interleave(grouped, rows, pair, copy):
             planes = slice(2 * pair, 2 * pair + 2)
@@ -142,13 +145,11 @@ def tile_picked_respelled_store_one_ladder_one_plain_kernel(
         def spell(t):
             nc.scalar.activation(xcd[t][:], table[t][:].indirect(list1[:]), COPY, scale=ga_t[:, t : t + 1])
 
-        for t in range(PACK - 1):
+        xc_first = keep.tile([P, PACK, HALF], BF16, name="xc_first", align_bytes=64)
+        for t in range(PACK):
             spell(t)
-        xc_first = keep.tile([P, PACK, HALF], BF16, name="xc_first", tag="ta2", align_bytes=64)
-        for t in range(PACK - 1):
+        for t in range(PACK):
             fetch_xc(xc_first, t, 0)
-        spell(PACK - 1)
-        fetch_xc(xc_first, PACK - 1, 0)
         xc_second = keep.tile([P, PACK, HALF], BF16, name="xc_second", tag="ta3", align_bytes=64)
         for t in range(PACK):
             fetch_xc(xc_second, t, 1)

from contextlib import ExitStack

import concourse.mybir as mybir

K, J, R, T, U, F, C, O, S, N = 512, 256, 512, 1024, 512, 1024, 512, 128, 256, 256
FLOPS = 2 * K * R * J + 2 * R * N * O

F32 = mybir.dt.float32
BF16 = mybir.dt.bfloat16
I32 = mybir.dt.int32
U32 = mybir.dt.uint32
U16 = mybir.dt.uint16
U8 = mybir.dt.uint8
FP8X4 = mybir.dt.float8_e4m3fn_x4
FP4X4 = mybir.dt.float4_e2m1fn_x4
COPY = mybir.ActivationFunctionType.Copy
MAX = mybir.AluOpType.max

P = 128
PACK = 4
QUADS = 4
LANES = 16
HALF = J // 2


def tile_picked_respelled_store_one_ladder_one_plain_kernel(
    tc, ta, ga, gb, wt_words, wt_scales, sa, sb, sd, wb_words, wb_scales,
    offs, offs2, offs3, offs4, offs5, offs6, offs7, out,
):
    nc = tc.nc
    with ExitStack() as ctx:
        keep = ctx.enter_context(tc.tile_pool(name="keep", bufs=1))
        psum = ctx.enter_context(tc.psum_pool(name="psum", bufs=1))

        def load_list(name, source):
            tile = keep.tile(list(source.shape), U16, name=name)
            nc.sync.dma_start(tile[:], source)
            return tile

        def load_rowwise(name, source, queue):
            tile = keep.tile([P, PACK], F32, name=name)
            queue.dma_start(tile[:], source.rearrange("(p t) o -> p (t o)", t=PACK))
            return tile

        ta_rows = ta.rearrange("(p t) c -> p t c", t=PACK)

        def load_ta(t):
            tile = keep.tile([P, T], F32, name="ta%d" % t, tag="ta%d" % t, align_bytes=64)
            nc.sync.dma_start(tile[:], ta_rows[:, t, :])
            return tile

        board = [keep.tile([P, C], F32, name="board%d" % t) for t in range(PACK)]
        wt_scale_table = keep.tile([P, F], U8, name="wt_scale_table", align_bytes=64)
        wb_scale = keep.tile([P, N], U8, name="wb_scale", align_bytes=64)
        nc.vector.memset(wt_scale_table[:].bitcast(I32), 0)
        nc.vector.memset(wb_scale[:].bitcast(I32), 0)
        for t in range(PACK):
            nc.vector.memset(board[t][:], 0.0)

        warm_in = keep.tile([P, 1], F32, name="warm_in")
        warm_out = keep.tile([P, 1], F32, name="warm_out")
        nc.gpsimd.memset(warm_in[:], 0.0)
        nc.scalar.activation(warm_out[:], warm_in[:], COPY)

        table = [load_ta(0)]
        list1 = load_list("list1", offs)
        ga_t = load_rowwise("ga_t", ga, nc.scalar)
        wt_scale_rows = keep.tile([4, QUADS, F // 4], I32, name="wt_scale_rows")
        nc.sync.dma_start(wt_scale_rows[:], wt_scales[0].bitcast(I32).rearrange("(q i) c -> i q c", i=4))
        list3 = load_list("list3", offs3)
        table.extend([load_ta(1), load_ta(2)])
        wt_word_table = keep.tile([P, F], U16, name="wt_word_table", align_bytes=64)
        nc.sync.dma_start(wt_word_table[:].bitcast(I32), wt_words[0].bitcast(I32))
        list2 = load_list("list2", offs2)
        gb_rows = gb.rearrange("(p t) o -> p (t o)", t=PACK)
        gb_pair = [keep.tile([P, 2], F32, name="gb_pair%d" % u) for u in range(2)]
        nc.sync.dma_start(gb_pair[0][:], gb_rows[:, 0:2])
        table.append(load_ta(3))
        nc.sync.dma_start(gb_pair[1][:], gb_rows[:, 2:4])
        list4 = load_list("list4", offs4)
        list5 = load_list("list5", offs5)
        list6 = load_list("list6", offs6)
        list7 = load_list("list7", offs7)
        sa_t = load_rowwise("sa_t", sa, nc.sync)
        sb_t = load_rowwise("sb_t", sb, nc.sync)
        sd_t = load_rowwise("sd_t", sd, nc.sync)
        wb_code = keep.tile([P, N], I32, name="wb_code", align_bytes=64)
        nc.sync.dma_start(wb_code[:], wb_words[0].rearrange("p n t -> p (n t)").bitcast(I32))
        for q in range(QUADS):
            nc.sync.dma_start(
                wb_scale[32 * q : 32 * q + 4, :].bitcast(I32), wb_scales[0, 4 * q : 4 * q + 4, :].bitcast(I32)
            )

        wt_picked = keep.tile([P, R], U16, name="wt_picked", align_bytes=64)
        nc.vector.tensor_copy(wt_picked[:], wt_word_table[:].indirect(list3[:]))
        wt_code = keep.tile([P, 2 * R], U8, name="wt_code", align_bytes=64)
        nc.vector.tensor_copy(
            wt_code[:].rearrange("p (t m b) -> p t m b", t=PACK, b=2),
            wt_picked[:].bitcast(U8).rearrange("p (m t b) -> p t m b", t=PACK, b=2),
        )
        for q in range(QUADS):
            nc.vector.tensor_copy(wt_scale_table[32 * q : 32 * q + 4, :].bitcast(I32), wt_scale_rows[:, q, :])
        wt_scale = keep.tile([P, R], U8, name="wt_scale", align_bytes=64)
        nc.vector.tensor_copy(
            wt_scale[:].rearrange("p (t m) -> p m t", t=PACK), wt_scale_table[:].indirect(list3[:])
        )

        xcd = [keep.tile([P, U], F32, name="xcd%d" % t) for t in range(PACK)]

        def fetch_xc(rows, t, h):
            cols = slice(h * HALF // LANES, (h + 1) * HALF // LANES)
            nc.scalar.activation(rows[:, t, :], xcd[t][:].indirect(list2[:, cols]), COPY, scale=gb_pair[t // 2][:, t % 2 : t % 2 + 1])

        def interleave(grouped, rows, pair, copy):
            planes = slice(2 * pair, 2 * pair + 2)
            copy(grouped[:, :, planes], rows[:, planes, :].rearrange("p t c -> p c t"))

        def quantize(name, grouped, width, tag):
            code = keep.tile([P, width], U32, name=name + "_code", tag=tag, align_bytes=64)
            scale = keep.tile([P, width], U8, name=name + "_scale", align_bytes=64)
            nc.vector.quantize_mx(code[:].bitcast(FP8X4), scale[:], grouped[:].rearrange("p c t -> p (c t)"))
            return code, scale

        def first_product(h, code, scale):
            first = psum.tile([P, HALF], F32, name="first%d" % h)
            rest = psum.tile([P, PACK - 1, HALF], F32, name="rest%d" % h)
            for t in range(PACK):
                nc.tensor.matmul_mx(
                    first[:] if t == 0 else rest[:, t - 1, :],
                    lhsT=wt_code[:, 2 * P * t : 2 * P * (t + 1)].bitcast(FP4X4),
                    lhsT_scale=wt_scale[:, P * t : P * (t + 1)],
                    rhs=code[:].bitcast(FP8X4),
                    rhs_scale=scale[:],
                    start=True,
                    stop=True,
                )
            return first, rest

        def scatter_half(t, h, values):
            nc.vector.tensor_copy(board[t][:].indirect(list4[:, h * HALF // LANES : (h + 1) * HALF // LANES]), values)

        hidden = keep.tile([P, PACK, J], F32, name="hidden")
        early, late = slice(0, HALF), slice(HALF, J)

        def spell(t):
            nc.scalar.activation(xcd[t][:], table[t][:].indirect(list1[:]), COPY, scale=ga_t[:, t : t + 1])

        xc_first = keep.tile([P, PACK, HALF], BF16, name="xc_first", align_bytes=64)
        for t in range(PACK):
            spell(t)
        for t in range(PACK):
            fetch_xc(xc_first, t, 0)
        xc_second = keep.tile([P, PACK, HALF], BF16, name="xc_second", tag="ta3", align_bytes=64)
        for t in range(PACK):
            fetch_xc(xc_second, t, 1)

        grouped = keep.tile([P, HALF, PACK], BF16, name="xc0_grouped", tag="xc_grouped", align_bytes=64)
        interleave(grouped, xc_first, 0, nc.vector.tensor_copy)
        interleave(grouped, xc_first, 1, nc.vector.tensor_copy)
        first, rest = first_product(0, *quantize("xc0", grouped, HALF, "xc0_code"))
        grouped = keep.tile([P, HALF, PACK], BF16, name="xc1_grouped", tag="xc_grouped", align_bytes=64)
        interleave(grouped, xc_second, 0, nc.vector.tensor_copy)
        interleave(grouped, xc_second, 1, nc.scalar.copy)
        opener = keep.tile([P, HALF], F32, name="opener", tag="opener", align_bytes=64)
        nc.vector.tensor_copy(opener[:], first[:])
        scatter_half(0, 0, opener[:])
        nc.scalar.copy(hidden[:, 1:, early], rest[:])
        first, rest = first_product(1, *quantize("xc1", grouped, HALF, "opener"))
        nc.scalar.copy(hidden[:, 0, late], first[:])
        nc.scalar.copy(hidden[:, 1:, late], rest[:])
        scatter_half(1, 0, hidden[:, 1, early])
        scatter_half(0, 1, hidden[:, 0, late])
        scatter_half(1, 1, hidden[:, 1, late])
        for t in range(2, PACK):
            nc.vector.tensor_copy(board[t][:].indirect(list4[:]), hidden[:, t, :])

        own = keep.tile([P, PACK, S], F32, name="own")
        shared = keep.tile([P, PACK, S], F32, name="shared")
        for t in range(PACK):
            nc.scalar.activation(own[:, t, :], board[t][:].indirect(list5[:]), COPY, scale=sa_t[:, t : t + 1])
            nc.scalar.activation(shared[:, t, :], board[t][:].indirect(list6[:]), COPY, scale=sb_t[:, t : t + 1])
        kept = [keep.tile([P, S], F32, name="kept%d" % t) for t in range(PACK)]
        for t in range(PACK):
            nc.vector.tensor_tensor(kept[t][:], own[:, t, :], shared[:, t, :], MAX)
        hid = keep.tile([P, PACK, O], BF16, name="hid", align_bytes=64)
        for t in range(PACK):
            nc.scalar.activation(hid[:, t, :], kept[t][:].indirect(list7[:]), COPY, scale=sd_t[:, t : t + 1])

        grouped = keep.tile([P, O, PACK], BF16, name="hid_grouped", align_bytes=64)
        interleave(grouped, hid, 0, nc.vector.tensor_copy)
        interleave(grouped, hid, 1, nc.vector.tensor_copy)
        code, scale = quantize("hid", grouped, O, "hid_code")
        for b in range(N // P):
            acc = psum.tile([P, O], F32, name="y%d" % b)
            nc.tensor.matmul_mx(
                acc[:],
                lhsT=wb_code[:, P * b : P * (b + 1)].bitcast(FP8X4),
                lhsT_scale=wb_scale[:, P * b : P * (b + 1)],
                rhs=code[:].bitcast(FP8X4),
                rhs_scale=scale[:],
                start=True,
                stop=True,
            )
            result = keep.tile([P, O], F32, name="result%d" % b)
            if b == 0:
                nc.vector.tensor_copy(result[:], acc[:])
                nc.sync.dma_start(out[P * b : P * (b + 1), :], result[:])
            else:
                nc.scalar.copy(result[:], acc[:])
                nc.scalar.dma_start(out[P * b : P * (b + 1), :], result[:])
